import numpy as np
import ml_dtypes


def mxq(x, axis, fmt="e4m3"):
    dtype, down = {"e4m3": (ml_dtypes.float8_e4m3fn, 7), "e5m2": (ml_dtypes.float8_e5m2, 14)}[fmt]
    v = np.moveaxis(np.asarray(x, np.float32).astype(ml_dtypes.bfloat16).astype(np.float64), axis, -1)
    blocks = v.reshape(v.shape[:-1] + (-1, 32))
    amax = np.abs(blocks).max(-1, keepdims=True)
    byte = np.maximum(np.where(amax > 0, np.frexp(amax)[1] - 1 + 127, 0) - down, 1)
    scale = np.exp2(byte - 127.0)
    codes = (blocks / scale).astype(np.float32).astype(dtype).astype(np.float64)
    return np.moveaxis((codes * scale).reshape(v.shape), -1, axis)


WIDE = False


def mx_kscale(k):
    if not WIDE:
        return np.ones(k)
    levels = np.array([10, -10, 5, -5, 0])
    if k % 512:
        return np.exp2(np.random.permutation(np.resize(levels, k // 32))).repeat(32)
    a = np.empty((k // 512, 16))
    for p in range(k // 512):
        a[p, :8] = np.random.permutation(np.resize(levels, 8))
        for g in range(8):
            far = levels[np.abs(levels - a[p, g]) >= 10]
            a[p, g + 8] = far[np.random.randint(len(far))]
    return np.exp2(a.ravel()).repeat(32)


def f64(x):
    return np.asarray(x).astype(np.float64)


def striped(idx):
    return np.tile(idx.reshape(-1, 16).T, (8, 1)).astype(np.uint16)


def unstriped(offs):
    return offs[:16].T.reshape(-1).astype(np.int64)


E2M1 = np.array([0.0, 0.5, 1.0, 1.5, 2.0, 3.0, 4.0, 6.0, -0.0, -0.5, -1.0, -1.5, -2.0, -3.0, -4.0, -6.0])


def pack_weight(w, fmt):
    k, n = w.shape
    w = f64(np.asarray(w, np.float32).astype(ml_dtypes.bfloat16)).reshape(k // 32, 32, n)
    amax = np.abs(w).max(1)
    if fmt == "e4m3":
        byte = np.frexp(amax)[1] - 1 + 127 - 7
    else:
        mant, ex = np.frexp(amax / 6.0)
        byte = np.where(mant > 0.5, ex, ex - 1) + 127
    byte = np.clip(np.where(amax > 0, byte, 1), 1, 254)
    scaled = (w * np.exp2(127.0 - byte)[:, None, :]).reshape(k, n).astype(np.float32)
    by_word = np.ascontiguousarray(scaled.reshape(k // 512, 128, 4, n).transpose(0, 1, 3, 2))
    if fmt == "e4m3":
        words = by_word.astype(ml_dtypes.float8_e4m3fn).view(np.uint8)
    else:
        c = by_word.astype(ml_dtypes.float4_e2m1fn).view(np.uint8) & 0xF
        words = (c[..., 0::2] | (c[..., 1::2] << 4)).reshape(k // 512, 128, 2 * n)
    return np.ascontiguousarray(words), np.ascontiguousarray(byte.astype(np.uint8).reshape(k // 512, 16, n))


def unpack_weight(words, scales, fmt):
    g, _, n = scales.shape
    words = np.ascontiguousarray(words).reshape(g, 128, n, -1)
    if fmt == "e4m3":
        vals = words.view(ml_dtypes.float8_e4m3fn).astype(np.float64)
    else:
        nib = np.empty((g, 128, n, 4), np.uint8)
        nib[..., 0::2] = words & 0xF
        nib[..., 1::2] = words >> 4
        vals = E2M1[nib]
    vals = vals * np.repeat(np.exp2(scales.astype(np.float64) - 127.0), 8, axis=1)[..., None]
    return vals.transpose(0, 1, 3, 2).reshape(g * 512, n)


def gelu(v):
    return 0.5 * v * (1.0 + np.tanh(np.sqrt(2.0 / np.pi) * (v + 0.044715 * v**3)))


K, H, T, S, T2, P, T3, S2 = 1536, 1024, 2048, 512, 1024, 512, 2048, 1024

def setup_inputs():
    n = np.random.standard_normal
    s = mx_kscale(K)[:, None]
    u = mx_kscale(H)[:, None]
    tab_words, tab_scales = pack_weight(n((K, T)) * s, "e4m3")
    tab2_words, tab2_scales = pack_weight(n((H, T3)) / u / np.sqrt(H), "e4m3")
    w4_words, w4_scales = pack_weight(1.4 * n((K, H)) / s / np.sqrt(K), "e2m1")
    return {
        "tab_words": tab_words, "tab_scales": tab_scales,
        "tab2_words": tab2_words, "tab2_scales": tab2_scales,
        "w4_words": w4_words, "w4_scales": w4_scales,
        "w1": (0.52 * n((K, H)) / s / np.sqrt(K)).astype(np.float32),
        "gain": (2.0 * np.exp(0.3 * n(H)) * u[:, 0]).astype(np.float32),
        "wgs": np.exp(0.3 * n((128, S))).astype(np.float32),
        "page0": (n((H, T2)) * u).astype(np.float32),
        "cls": ((0.8 * n((H, P)) - 0.6) * u).astype(np.float32),
        "cand": (1.8 * np.exp(0.4 * n(S2))).astype(np.float32),
        "offs": striped(np.random.permutation(T)[:S]),
        "offs2": striped(np.random.permutation(T3)[:S2]),
        "offs3": striped(np.random.permutation(T2)[:S]),
        "offs4": striped(np.random.permutation(T2)[:P]),
    }

def reference(tab_words, tab_scales, tab2_words, tab2_scales, w4_words, w4_scales, w1, gain, wgs, page0, cls, cand, offs, offs2, offs3, offs4):
    v = unpack_weight(tab_words, tab_scales, "e4m3")[:, unstriped(offs)]
    v2 = unpack_weight(tab2_words, tab2_scales, "e4m3")[:, unstriped(offs2)]
    w4 = unpack_weight(w4_words, w4_scales, "e2m1")
    content = np.tanh(w4.T @ v)
    phase = np.cos(mxq(f64(w1), 0, "e4m3").T @ v)
    h = content * phase * f64(gain)[:, None]
    page = f64(page0).copy()
    page[:, unstriped(offs3)] = np.tile(f64(wgs), (H // 128, 1)) * h
    x = np.maximum(page[:, unstriped(offs4)], f64(cls))
    e = v2.T @ mxq(x, 0, "e4m3")
    z = e * f64(cand)[:, None]
    return 1.0 / (1.0 + np.exp(-z))

@@ -1,0 +1,233 @@
+import math
+from contextlib import ExitStack
+
+import concourse.mybir as mybir
+from concourse.masks import make_identity
+
+K, H, T, S, T2, PX, T3, S2 = 1536, 1024, 2048, 512, 1024, 512, 2048, 1024
+FLOPS = 2 * (2 * K * H * S + H * S2 * PX)
+
+F32 = mybir.dt.float32
+BF16 = mybir.dt.bfloat16
+I32 = mybir.dt.int32
+U32 = mybir.dt.uint32
+U16 = mybir.dt.uint16
+U8 = mybir.dt.uint8
+FP8X4 = mybir.dt.float8_e4m3fn_x4
+FP4X4 = mybir.dt.float4_e2m1fn_x4
+ALU = mybir.AluOpType
+ACT = mybir.ActivationFunctionType
+
+P = 128
+KP = K // 512
+HP = H // 512
+CHUNKS = ((0, 256), (256, 512))
+
+
+def tile_list_prior_art_scores_kernel(tc, tab_words, tab_scales, tab2_words, tab2_scales, w4_words, w4_scales,
+                                                w1, gain, wgs, page0, cls, cand, offs, offs2, offs3, offs4, out):
+    nc = tc.nc
+    with ExitStack() as ctx:
+        lists = ctx.enter_context(tc.tile_pool(name="lists", bufs=1))
+        keep = ctx.enter_context(tc.tile_pool(name="keep", bufs=1))
+        ring = ctx.enter_context(tc.tile_pool(name="ring", bufs=2))
+        stage = ctx.enter_context(tc.tile_pool(name="stage", bufs=1))
+        psum = ctx.enter_context(tc.psum_pool(name="psum", bufs=8))
+
+        idx = lists.tile([P, S // 16], U16, name="idx")
+        idx2 = lists.tile([P, S2 // 16], U16, name="idx2")
+        idx3 = lists.tile([P, S // 16], U16, name="idx3")
+        idx4 = lists.tile([P, PX // 16], U16, name="idx4")
+
+        ident = keep.tile([P, P], F32, name="ident")
+        make_identity(nc, ident[:])
+
+        def packed_scales(name, scales, passes, width):
+            plane = keep.tile([P, width], U8, name=name, align_bytes=64)
+            nc.vector.memset(plane[:].bitcast(I32), 0)
+            for q in range(4):
+                nc.sync.dma_start(out=plane[32 * q : 32 * q + 4 * passes, :].bitcast(I32),
+                                  in_=scales[:, 4 * q : 4 * q + 4, :].bitcast(I32))
+            return plane
+
+        def spread_scales(name, scales, width, engine):
+            planes = keep.tile([P, KP, width], U8, name=name, align_bytes=64)
+            engine.memset(planes[:].bitcast(I32), 0)
+            for q in range(4):
+                nc.sync.dma_start(out=planes[32 * q : 32 * q + 4, :, :].bitcast(I32),
+                                  in_=scales[:, 4 * q : 4 * q + 4, :].rearrange("a r n -> r a n").bitcast(I32))
+            return planes
+
+        def load_words(name, words, a):
+            tile = keep.tile([P, words.shape[2]], I32, name="%s%d" % (name, a), align_bytes=64)
+            nc.sync.dma_start(out=tile[:], in_=words[a].rearrange("p n i -> p (n i)").bitcast(I32))
+            return tile
+
+        def load_w1(a, b):
+            raw = ring.tile([P, 4, 512], F32, name="w1_raw", bufs=3)
+            nc.sync.dma_start(out=raw[:], in_=w1[512 * a : 512 * (a + 1), 512 * b : 512 * (b + 1)].rearrange("(p j) c -> p j c", j=4))
+            return raw
+
+        def load_page(b, t):
+            tile = keep.tile([P, T2], F32, name="page%d" % (4 * b + t))
+            nc.sync.dma_start(out=tile[:], in_=page0[512 * b : 512 * (b + 1), :].rearrange("(p t) c -> p t c", t=4)[:, t, :])
+            return tile
+
+        def load_cls(b):
+            tile = keep.tile([P, 4, PX], F32, name="cls%d" % b)
+            nc.sync.dma_start(out=tile[:], in_=cls[512 * b : 512 * (b + 1), :].rearrange("(p t) j -> p t j", t=4))
+            return tile
+
+        for tile, src in ((idx, offs), (idx2, offs2), (idx3, offs3), (idx4, offs4)):
+            nc.sync.dma_start(tile[:], src)
+        w4_raw = []
+        for a in range(KP):
+            raw4 = keep.tile([P, 2 * H], U8, name="w4_raw%d" % a)
+            nc.sync.dma_start(out=raw4[:].bitcast(I32), in_=w4_words[a].bitcast(I32))
+            w4_raw.append(raw4)
+        tab_sb = [load_words("tab", tab_words, 0)]
+        w4s_raw = spread_scales("w4s_raw", w4_scales, H, nc.vector)
+        tab_sb.append(load_words("tab", tab_words, 1))
+        tabs_sb = spread_scales("tabs", tab_scales, T, nc.gpsimd)
+        tab_sb.append(load_words("tab", tab_words, 2))
+        tab2_sb = [load_words("tabb", tab2_words, 0)]
+        tab2s_sb = packed_scales("tabbs", tab2_scales, HP, T3)
+        w1_raw = {}
+        for a in range(KP):
+            w1_raw[a, 0] = load_w1(a, 0)
+        gain_sb = keep.tile([P, HP, 4], F32, name="gain_sb")
+        nc.sync.dma_start(out=gain_sb[:], in_=gain.rearrange("(b p t) -> p b t", b=HP, t=4))
+        wgs_sb = keep.tile([P, 4, S], F32, name="wgs_sb")
+        for q in range(4):
+            nc.sync.dma_start(out=wgs_sb[32 * q : 32 * (q + 1), :, :], in_=wgs.rearrange("(p t) j -> p t j", t=4))
+        pages = [load_page(0, 0)]
+        tab2_sb.append(load_words("tabb", tab2_words, 1))
+        pages.extend(load_page(0, t) for t in range(1, 4))
+
+        w4_sb, w4s, vw, vs = [], [], [], []
+        for a in range(KP):
+            dealt = keep.tile([P, 2 * H], U8, name="w4_%d" % a, align_bytes=64)
+            nc.vector.tensor_copy(out=dealt[:].bitcast(U16).rearrange("p (b t m i) -> p b m t i", b=HP, t=4, i=8),
+                                  in_=w4_raw[a][:].bitcast(U16).rearrange("p (b m i t) -> p b m t i", b=HP, t=4, i=8))
+            w4_sb.append(dealt)
+        for a in range(KP):
+            words = keep.tile([P, S], U32, name="vw%d" % a, align_bytes=64)
+            nc.vector.tensor_copy(words[:], tab_sb[a][:].bitcast(U32).indirect(idx[:]))
+            vw.append(words)
+            plane = keep.tile([P, S], U8, name="vs%d" % a, align_bytes=64)
+            nc.vector.tensor_copy(plane[:], tabs_sb[:, a, :].indirect(idx[:]))
+            vs.append(plane)
+            dealt = keep.tile([P, H], U8, name="w4s%d" % a, align_bytes=64)
+            nc.vector.tensor_copy(out=dealt[:].rearrange("p (b t m i) -> p b m t i", b=HP, t=4, i=16),
+                                  in_=w4s_raw[:, a, :].rearrange("p (b m i t) -> p b m t i", b=HP, t=4, i=16))
+            w4s.append(dealt)
+
+        amp = []
+
+        def content():
+            accs = [psum.tile([P, S], F32, name="acc") for bt in range(4 * HP)]
+            for a in range(KP):
+                for bt in range(4 * HP):
+                    nc.tensor.matmul_mx(out=accs[bt][:], lhsT=w4_sb[a][:, 256 * bt : 256 * (bt + 1)].bitcast(FP4X4),
+                                        lhsT_scale=w4s[a][:, P * bt : P * (bt + 1)], rhs=vw[a][:].bitcast(FP8X4),
+                                        rhs_scale=vs[a][:], start=(a == 0), stop=(a == KP - 1))
+            for bt in range(4 * HP):
+                tile = keep.tile([P, S], F32, name="amp", bufs=4 * HP)
+                nc.scalar.activation(out=tile[:], in_=accs[bt][:], func=ACT.Tanh)
+                amp.append(tile)
+
+        def weigh(bt):
+            nc.vector.scalar_tensor_tensor(out=amp[bt][:], in0=amp[bt][:], scalar=gain_sb[:, bt // 4, bt % 4 : bt % 4 + 1],
+                                           in1=wgs_sb[:, bt % 4, :], op0=ALU.mult, op1=ALU.mult)
+
+        def quantise_w1(a, b, split):
+            grouped = stage.tile([P, 2048], BF16, name="grouped%d%d" % (a, b), align_bytes=64, offset=4096 * ((a + b) % 2))
+            dst = grouped[:].rearrange("p (t m j) -> p m t j", t=4, j=4)
+            raw = w1_raw[a, b][:].rearrange("p j (m t) -> p m t j", t=4)
+            if split < P:
+                nc.vector.tensor_copy(out=dst[:, split:], in_=raw[:, split:])
+            nc.scalar.copy(out=dst[:, :split], in_=raw[:, :split])
+            codes = keep.tile([P, 512], U32, name="w1c%d%d" % (a, b), align_bytes=64)
+            scales = keep.tile([P, 512], U8, name="w1s%d%d" % (a, b), align_bytes=64)
+            nc.vector.quantize_mx(out=codes[:].bitcast(FP8X4), scales=scales[:], in_=grouped[:])
+            return codes, scales
+
+        def phase_and_scatter(b, w1q):
+            accs = [psum.tile([P, S], F32, name="acc") for t in range(4)]
+            for a in range(KP):
+                codes, scales = w1q[a]
+                for t in range(4):
+                    for c in range(4):
+                        nc.tensor.matmul_mx(out=accs[t][:, P * c : P * (c + 1)], lhsT=vw[a][:, P * c : P * (c + 1)].bitcast(FP8X4),
+                                            lhsT_scale=vs[a][:, P * c : P * (c + 1)], rhs=codes[:, P * t : P * (t + 1)].bitcast(FP8X4),
+                                            rhs_scale=scales[:, P * t : P * (t + 1)], start=(a == 0 and c == 0),
+                                            stop=(a == KP - 1 and c == 3))
+            for t in range(4):
+                turns = ring.tile([P, S], F32, name="turns")
+                nc.scalar.activation(out=turns[:], in_=accs[t][:], func=ACT.Abs, scale=1.0 / (2.0 * math.pi))
+                whole = ring.tile([P, S], U32, name="whole")
+                nc.scalar.activation(out=whole[:], in_=turns[:], func=ACT.Copy, bias=0.25)
+                shift = ring.tile([P, S], F32, name="shift")
+                nc.scalar.activation(out=shift[:], in_=whole[:], func=ACT.Copy, scale=-1.0, bias=0.25)
+                reduced = psum.tile([P, S], F32, name="acc")
+                for c in range(4):
+                    cols = slice(P * c, P * (c + 1))
+                    nc.tensor.matmul(reduced[:, cols], lhsT=turns[:, cols], rhs=ident[:], start=True, stop=False, is_transpose=True)
+                    nc.tensor.matmul(reduced[:, cols], lhsT=shift[:, cols], rhs=ident[:], start=False, stop=True, is_transpose=True)
+                cosine = ring.tile([P, S], F32, name="cosine", bufs=4)
+                nc.scalar.activation(out=cosine[:], in_=reduced[:], func=ACT.Sin, scale=2.0 * math.pi)
+                nc.vector.tensor_tensor(pages[4 * b + t][:].indirect(idx3[:]), amp[4 * b + t][:], cosine[:], ALU.mult)
+
+        def examine(b, lo, hi):
+            n = hi - lo
+            picked = stage.tile([P, 4, n], F32, name="picked%d%d" % (b, lo), align_bytes=64, offset=32 * lo)
+            for t in range(4):
+                nc.vector.tensor_copy(picked[:, t, :], pages[4 * b + t][:].indirect(idx4[:, lo // 16 : hi // 16]))
+            x = stage.tile([P, 4 * n], BF16, name="x%d%d" % (b, lo), align_bytes=64, offset=8192 - 32 * lo)
+            nc.vector.tensor_tensor(x[:].rearrange("p (c i t) -> p c t i", t=4, i=4),
+                                    picked[:].rearrange("p t (c i) -> p c t i", i=4),
+                                    cls_sb[b][:, :, lo:hi].rearrange("p t (c i) -> p c t i", i=4), ALU.max)
+            nc.vector.quantize_mx(out=xw[b][:, lo:hi].bitcast(FP8X4), scales=xs[b][:, lo:hi], in_=x[:])
+
+        def gather_tab2(a):
+            words = keep.tile([P, S2], U32, name="v2w%d" % a, align_bytes=64)
+            nc.vector.tensor_copy(words[:], tab2_sb[a][:].bitcast(U32).indirect(idx2[:]))
+            return words
+
+        w1q0 = [quantise_w1(a, 0, 64 if a == KP - 1 else P) for a in range(KP)]
+        content()
+        for bt in range(4 * HP):
+            weigh(bt)
+        v2s = keep.tile([P, S2], U8, name="v2s", align_bytes=64)
+        nc.vector.tensor_copy(v2s[:], tab2s_sb[:].indirect(idx2[:]))
+        v2w = [gather_tab2(a) for a in range(HP)]
+
+        for a in range(KP):
+            w1_raw[a, 1] = load_w1(a, 1)
+        cls_sb = [load_cls(0)]
+        pages.extend(load_page(1, t) for t in range(4))
+        cls_sb.append(load_cls(1))
+        cand_sb = keep.tile([P, S2 // P], F32, name="cand_sb")
+        with nc.allow_non_contiguous_dma(reason="one factor to a partition"):
+            nc.sync.dma_start(out=cand_sb[:], in_=cand.rearrange("(m p) -> p m", p=P))
+
+        xw = [keep.tile([P, PX], U32, name="xw%d" % b, align_bytes=64) for b in range(HP)]
+        xs = [keep.tile([P, PX], U8, name="xs%d" % b, align_bytes=64) for b in range(HP)]
+
+        phase_and_scatter(0, w1q0)
+        w1q1 = [quantise_w1(a, 1, P) for a in range(KP)]
+        examine(0, 0, PX)
+        phase_and_scatter(1, w1q1)
+        out_rows = out.rearrange("(m p) j -> p m j", p=P)
+        for lo, hi in CHUNKS:
+            examine(1, lo, hi)
+            for m0 in range(0, S2 // P, 2):
+                score = keep.tile([P, 2, hi - lo], F32, name="amp", bufs=4 * HP)
+                for m in range(m0, m0 + 2):
+                    acc = psum.tile([P, hi - lo], F32, name="acc")
+                    for b in range(HP):
+                        nc.tensor.matmul_mx(out=acc[:], lhsT=v2w[b][:, P * m : P * (m + 1)].bitcast(FP8X4),
+                                            lhsT_scale=v2s[4 * b :, P * m : P * (m + 1)], rhs=xw[b][:, lo:hi].bitcast(FP8X4),
+                                            rhs_scale=xs[b][:, lo:hi], start=(b == 0), stop=(b == HP - 1))
+                    nc.scalar.activation(out=score[:, m - m0, :], in_=acc[:], func=ACT.Sigmoid, scale=cand_sb[:, m : m + 1])
+                nc.sync.dma_start(out=out_rows[:, m0 : m0 + 2, lo:hi], in_=score[:])

@@ -142,8 +142,8 @@ def tile_list_prior_art_scores_kernel(tc, tab_words, tab_scales, tab2_words, tab
 
         def quantise_w1(a, b, split):
             grouped = stage.tile([P, 2048], BF16, name="grouped%d%d" % (a, b), align_bytes=64, offset=4096 * ((a + b) % 2))
-            dst = grouped[:].rearrange("p (t m j) -> p m t j", t=4, j=4)
-            raw = w1_raw[a, b][:].rearrange("p j (m t) -> p m t j", t=4)
+            dst = grouped[:].rearrange("p (m i j) -> p m j i", i=4, j=4)
+            raw = w1_raw[a, b][:].rearrange("p j (m i) -> p m j i", i=4)
             if split < P:
                 nc.vector.tensor_copy(out=dst[:, split:], in_=raw[:, split:])
             nc.scalar.copy(out=dst[:, :split], in_=raw[:, :split])
@@ -156,16 +156,16 @@ def tile_list_prior_art_scores_kernel(tc, tab_words, tab_scales, tab2_words, tab
             accs = [psum.tile([P, S], F32, name="acc") for t in range(4)]
             for a in range(KP):
                 codes, scales = w1q[a]
-                for t in range(4):
-                    for c in range(4):
-                        nc.tensor.matmul_mx(out=accs[t][:, P * c : P * (c + 1)], lhsT=vw[a][:, P * c : P * (c + 1)].bitcast(FP8X4),
-                                            lhsT_scale=vs[a][:, P * c : P * (c + 1)], rhs=codes[:, P * t : P * (t + 1)].bitcast(FP8X4),
-                                            rhs_scale=scales[:, P * t : P * (t + 1)], start=(a == 0 and c == 0),
-                                            stop=(a == KP - 1 and c == 3))
+                for c in range(4):
+                    nc.tensor.matmul_mx(out=accs[c][:], lhsT=vw[a][:, P * c : P * (c + 1)].bitcast(FP8X4),
+                                        lhsT_scale=vs[a][:, P * c : P * (c + 1)], rhs=codes[:].bitcast(FP8X4),
+                                        rhs_scale=scales[:], start=(a == 0), stop=(a == KP - 1))
             for t in range(4):
                 turns = ring.tile([P, S], F32, name="turns")
-                nc.scalar.activation(out=turns[:], in_=accs[t][:], func=ACT.Abs, scale=1.0 / (2.0 * math.pi))
-                whole = ring.tile([P, S], U32, name="whole")
+                for c in range(4):
+                    nc.scalar.activation(out=turns[:, P * c : P * (c + 1)], in_=accs[c][:, t::4], func=ACT.Abs,
+                                         scale=1.0 / (2.0 * math.pi))
+                whole = stage.tile([P, S], U32, name="whole%d%d" % (b, t), align_bytes=64, offset=12288 + 2048 * (t % 2))
                 nc.scalar.activation(out=whole[:], in_=turns[:], func=ACT.Copy, bias=0.25)
                 shift = ring.tile([P, S], F32, name="shift")
                 nc.scalar.activation(out=shift[:], in_=whole[:], func=ACT.Copy, scale=-1.0, bias=0.25)
@@ -180,13 +180,17 @@ def tile_list_prior_art_scores_kernel(tc, tab_words, tab_scales, tab2_words, tab
 
         def examine(b, lo, hi):
             n = hi - lo
-            picked = stage.tile([P, 4, n], F32, name="picked%d%d" % (b, lo), align_bytes=64, offset=32 * lo)
+            picked = stage.tile([P, 4, n], F32, name="picked%d%d" % (b, lo), align_bytes=64, offset=0)
+            larger = stage.tile([P, 4, n], BF16, name="larger%d%d" % (b, lo), align_bytes=64, offset=(4096 if b else 8192) + 8 * lo)
             for t in range(4):
                 nc.vector.tensor_copy(picked[:, t, :], pages[4 * b + t][:].indirect(idx4[:, lo // 16 : hi // 16]))
-            x = stage.tile([P, 4 * n], BF16, name="x%d%d" % (b, lo), align_bytes=64, offset=8192 - 32 * lo)
-            nc.vector.tensor_tensor(x[:].rearrange("p (c i t) -> p c t i", t=4, i=4),
-                                    picked[:].rearrange("p t (c i) -> p c t i", i=4),
-                                    cls_sb[b][:, :, lo:hi].rearrange("p t (c i) -> p c t i", i=4), ALU.max)
+            for t0, t1 in ((0, 3), (3, 4)):
+                nc.vector.tensor_tensor(larger[:, t0:t1, :], picked[:, t0:t1, :], cls_sb[b][:, t0:t1, lo:hi], ALU.max)
+            return larger
+
+        def quantise_x(b, lo, hi, larger, weave):
+            x = stage.tile([P, 4 * (hi - lo)], BF16, name="x%d%d" % (b, lo), align_bytes=64, offset=12288 + 8 * lo)
+            weave(out=x[:].rearrange("p (c i t) -> p c t i", t=4, i=4), in_=larger[:].rearrange("p t (c i) -> p c t i", i=4))
             nc.vector.quantize_mx(out=xw[b][:, lo:hi].bitcast(FP8X4), scales=xs[b][:, lo:hi], in_=x[:])
 
         def gather_tab2(a):
@@ -194,7 +198,7 @@ def tile_list_prior_art_scores_kernel(tc, tab_words, tab_scales, tab2_words, tab
             nc.vector.tensor_copy(words[:], tab2_sb[a][:].bitcast(U32).indirect(idx2[:]))
             return words
 
-        w1q0 = [quantise_w1(a, 0, 64 if a == KP - 1 else P) for a in range(KP)]
+        w1q0 = [quantise_w1(a, 0, 64) for a in range(KP)]
         content()
         for bt in range(4 * HP):
             weigh(bt)
@@ -216,11 +220,12 @@ def tile_list_prior_art_scores_kernel(tc, tab_words, tab_scales, tab2_words, tab
 
         phase_and_scatter(0, w1q0)
         w1q1 = [quantise_w1(a, 1, P) for a in range(KP)]
-        examine(0, 0, PX)
+        larger0 = examine(0, 0, PX)
         phase_and_scatter(1, w1q1)
+        quantise_x(0, 0, PX, larger0, nc.scalar.copy)
         out_rows = out.rearrange("(m p) j -> p m j", p=P)
         for lo, hi in CHUNKS:
-            examine(1, lo, hi)
+            quantise_x(1, lo, hi, examine(1, lo, hi), nc.scalar.copy if lo == 0 else nc.vector.tensor_copy)
             for m0 in range(0, S2 // P, 2):
                 score = keep.tile([P, 2, hi - lo], F32, name="amp", bufs=4 * HP)
                 for m in range(m0, m0 + 2):

@@ -32,7 +32,7 @@ def tile_list_prior_art_scores_kernel(tc, tab_words, tab_scales, tab2_words, tab
         keep = ctx.enter_context(tc.tile_pool(name="keep", bufs=1))
         ring = ctx.enter_context(tc.tile_pool(name="ring", bufs=2))
         stage = ctx.enter_context(tc.tile_pool(name="stage", bufs=1))
-        psum = ctx.enter_context(tc.psum_pool(name="psum", bufs=8))
+        psum = ctx.enter_context(tc.psum_pool(name="psum", bufs=4))
 
         idx = lists.tile([P, S // 16], U16, name="idx")
         idx2 = lists.tile([P, S2 // 16], U16, name="idx2")
@@ -63,6 +63,11 @@ def tile_list_prior_art_scores_kernel(tc, tab_words, tab_scales, tab2_words, tab
             nc.sync.dma_start(out=tile[:], in_=words[a].rearrange("p n i -> p (n i)").bitcast(I32))
             return tile
 
+        def load_w4(a):
+            tile = keep.tile([P, 2 * H], U8, name="w4_%d" % a, align_bytes=64)
+            nc.sync.dma_start(out=tile[:].bitcast(I32), in_=w4_words[a].bitcast(I32))
+            return tile
+
         def load_w1(a, b):
             raw = ring.tile([P, 4, 512], F32, name="w1_raw", bufs=3)
             nc.sync.dma_start(out=raw[:], in_=w1[512 * a : 512 * (a + 1), 512 * b : 512 * (b + 1)].rearrange("(p j) c -> p j c", j=4))
@@ -80,36 +85,27 @@ def tile_list_prior_art_scores_kernel(tc, tab_words, tab_scales, tab2_words, tab
 
         for tile, src in ((idx, offs), (idx2, offs2), (idx3, offs3), (idx4, offs4)):
             nc.sync.dma_start(tile[:], src)
-        w4_raw = []
-        for a in range(KP):
-            raw4 = keep.tile([P, 2 * H], U8, name="w4_raw%d" % a)
-            nc.sync.dma_start(out=raw4[:].bitcast(I32), in_=w4_words[a].bitcast(I32))
-            w4_raw.append(raw4)
+        gain_sb = keep.tile([P, HP, 4], F32, name="gain_sb")
+        nc.sync.dma_start(out=gain_sb[:], in_=gain.rearrange("(b p t) -> p b t", b=HP, t=4))
         tab_sb = [load_words("tab", tab_words, 0)]
-        w4s_raw = spread_scales("w4s_raw", w4_scales, H, nc.vector)
+        w4_sb = [load_w4(a) for a in range(KP - 1)]
+        tabs_sb = spread_scales("tabs", tab_scales, T, nc.vector)
         tab_sb.append(load_words("tab", tab_words, 1))
-        tabs_sb = spread_scales("tabs", tab_scales, T, nc.gpsimd)
+        w4s = spread_scales("w4s", w4_scales, H, nc.vector)
+        w4_sb.append(load_w4(KP - 1))
         tab_sb.append(load_words("tab", tab_words, 2))
-        tab2_sb = [load_words("tabb", tab2_words, 0)]
-        tab2s_sb = packed_scales("tabbs", tab2_scales, HP, T3)
         w1_raw = {}
         for a in range(KP):
             w1_raw[a, 0] = load_w1(a, 0)
-        gain_sb = keep.tile([P, HP, 4], F32, name="gain_sb")
-        nc.sync.dma_start(out=gain_sb[:], in_=gain.rearrange("(b p t) -> p b t", b=HP, t=4))
-        wgs_sb = keep.tile([P, 4, S], F32, name="wgs_sb")
-        for q in range(4):
-            nc.sync.dma_start(out=wgs_sb[32 * q : 32 * (q + 1), :, :], in_=wgs.rearrange("(p t) j -> p t j", t=4))
+        wgs_sb = keep.tile([P, S], F32, name="wgs_sb")
+        nc.sync.dma_start(out=wgs_sb[:], in_=wgs)
+        tab2_sb = [load_words("tabb", tab2_words, 0)]
+        tab2s_sb = packed_scales("tabbs", tab2_scales, HP, T3)
         pages = [load_page(0, 0)]
         tab2_sb.append(load_words("tabb", tab2_words, 1))
         pages.extend(load_page(0, t) for t in range(1, 4))
 
-        w4_sb, w4s, vw, vs = [], [], [], []
-        for a in range(KP):
-            dealt = keep.tile([P, 2 * H], U8, name="w4_%d" % a, align_bytes=64)
-            nc.vector.tensor_copy(out=dealt[:].bitcast(U16).rearrange("p (b t m i) -> p b m t i", b=HP, t=4, i=8),
-                                  in_=w4_raw[a][:].bitcast(U16).rearrange("p (b m i t) -> p b m t i", b=HP, t=4, i=8))
-            w4_sb.append(dealt)
+        vw, vs = [], []
         for a in range(KP):
             words = keep.tile([P, S], U32, name="vw%d" % a, align_bytes=64)
             nc.vector.tensor_copy(words[:], tab_sb[a][:].bitcast(U32).indirect(idx[:]))
@@ -117,43 +113,53 @@ def tile_list_prior_art_scores_kernel(tc, tab_words, tab_scales, tab2_words, tab
             plane = keep.tile([P, S], U8, name="vs%d" % a, align_bytes=64)
             nc.vector.tensor_copy(plane[:], tabs_sb[:, a, :].indirect(idx[:]))
             vs.append(plane)
-            dealt = keep.tile([P, H], U8, name="w4s%d" % a, align_bytes=64)
-            nc.vector.tensor_copy(out=dealt[:].rearrange("p (b t m i) -> p b m t i", b=HP, t=4, i=16),
-                                  in_=w4s_raw[:, a, :].rearrange("p (b m i t) -> p b m t i", b=HP, t=4, i=16))
-            w4s.append(dealt)
 
-        amp = []
+        turned = psum.tile([P, 4, P], F32, name="turn")
+        for c in range(4):
+            nc.tensor.transpose(turned[:, c, :], wgs_sb[:, P * c : P * (c + 1)], ident[:])
+        wgs_t = keep.tile([P, 4, 4, 32], F32, name="wgs_t")
+        nc.scalar.copy(out=wgs_t[:], in_=turned[:].rearrange("p c (m t) -> p c t m", t=4))
 
-        def content():
-            accs = [psum.tile([P, S], F32, name="acc") for bt in range(4 * HP)]
+        def content(b):
+            accs = [psum.tile([P, 512], F32, name=("wide", "turn")[b]) for c in range(4)]
             for a in range(KP):
-                for bt in range(4 * HP):
-                    nc.tensor.matmul_mx(out=accs[bt][:], lhsT=w4_sb[a][:, 256 * bt : 256 * (bt + 1)].bitcast(FP4X4),
-                                        lhsT_scale=w4s[a][:, P * bt : P * (bt + 1)], rhs=vw[a][:].bitcast(FP8X4),
-                                        rhs_scale=vs[a][:], start=(a == 0), stop=(a == KP - 1))
-            for bt in range(4 * HP):
-                tile = keep.tile([P, S], F32, name="amp", bufs=4 * HP)
-                nc.scalar.activation(out=tile[:], in_=accs[bt][:], func=ACT.Tanh)
-                amp.append(tile)
+                for c in range(4):
+                    nc.tensor.matmul_mx(out=accs[c][:], lhsT=vw[a][:, P * c : P * (c + 1)].bitcast(FP8X4),
+                                        lhsT_scale=vs[a][:, P * c : P * (c + 1)],
+                                        rhs=w4_sb[a][:, 1024 * b : 1024 * (b + 1)].bitcast(FP4X4),
+                                        rhs_scale=w4s[:, a, 512 * b : 512 * (b + 1)], start=(a == 0), stop=(a == KP - 1))
+            tiles = []
+            for c in range(4):
+                tile = keep.tile([P, 4, P], F32, name="tanh_t", bufs=4 * HP)
+                nc.scalar.activation(out=tile[:], in_=accs[c][:].rearrange("p (m t) -> p t m", t=4), func=ACT.Tanh)
+                tiles.append(tile)
+            return tiles
 
-        def weigh(bt):
-            nc.vector.scalar_tensor_tensor(out=amp[bt][:], in0=amp[bt][:], scalar=gain_sb[:, bt // 4, bt % 4 : bt % 4 + 1],
-                                           in1=wgs_sb[:, bt % 4, :], op0=ALU.mult, op1=ALU.mult)
+        def weigh(tiles):
+            for c in range(4):
+                view = tiles[c][:].rearrange("p t (q m) -> p t q m", q=4)
+                nc.vector.tensor_tensor(view, view, wgs_t[:, c, :, :].unsqueeze(2).to_broadcast([P, 4, 4, 32]), ALU.mult)
 
-        def quantise_w1(a, b, split):
+        def amplitude(b, t, tiles):
+            bank = psum.tile([P, S], F32, name="turn")
+            for c in range(4):
+                nc.tensor.transpose(bank[:, P * c : P * (c + 1)], tiles[c][:, t, :], ident[:])
+            tile = ring.tile([P, S], F32, name="amp", bufs=4)
+            nc.scalar.activation(out=tile[:], in_=bank[:], func=ACT.Copy, scale=gain_sb[:, b, t : t + 1])
+            return tile
+
+        def quantise_w1(a, b, weave):
             grouped = stage.tile([P, 2048], BF16, name="grouped%d%d" % (a, b), align_bytes=64, offset=4096 * ((a + b) % 2))
             dst = grouped[:].rearrange("p (m i j) -> p m j i", i=4, j=4)
             raw = w1_raw[a, b][:].rearrange("p j (m i) -> p m j i", i=4)
-            if split < P:
-                nc.vector.tensor_copy(out=dst[:, split:], in_=raw[:, split:])
-            nc.scalar.copy(out=dst[:, :split], in_=raw[:, :split])
+            weave(out=dst, in_=raw)
             codes = keep.tile([P, 512], U32, name="w1c%d%d" % (a, b), align_bytes=64)
             scales = keep.tile([P, 512], U8, name="w1s%d%d" % (a, b), align_bytes=64)
             nc.vector.quantize_mx(out=codes[:].bitcast(FP8X4), scales=scales[:], in_=grouped[:])
             return codes, scales
 
-        def phase_and_scatter(b, w1q):
-            accs = [psum.tile([P, S], F32, name="acc") for t in range(4)]
+        def phase_and_scatter(b, w1q, tiles):
+            accs = [psum.tile([P, 512], F32, name="wide") for c in range(4)]
             for a in range(KP):
                 codes, scales = w1q[a]
                 for c in range(4):
@@ -169,14 +175,15 @@ def tile_list_prior_art_scores_kernel(tc, tab_words, tab_scales, tab2_words, tab
                 nc.scalar.activation(out=whole[:], in_=turns[:], func=ACT.Copy, bias=0.25)
                 shift = ring.tile([P, S], F32, name="shift")
                 nc.scalar.activation(out=shift[:], in_=whole[:], func=ACT.Copy, scale=-1.0, bias=0.25)
-                reduced = psum.tile([P, S], F32, name="acc")
+                reduced = psum.tile([P, S], F32, name="turn")
                 for c in range(4):
                     cols = slice(P * c, P * (c + 1))
                     nc.tensor.matmul(reduced[:, cols], lhsT=turns[:, cols], rhs=ident[:], start=True, stop=False, is_transpose=True)
                     nc.tensor.matmul(reduced[:, cols], lhsT=shift[:, cols], rhs=ident[:], start=False, stop=True, is_transpose=True)
                 cosine = ring.tile([P, S], F32, name="cosine", bufs=4)
                 nc.scalar.activation(out=cosine[:], in_=reduced[:], func=ACT.Sin, scale=2.0 * math.pi)
-                nc.vector.tensor_tensor(pages[4 * b + t][:].indirect(idx3[:]), amp[4 * b + t][:], cosine[:], ALU.mult)
+                amp = amplitude(b, t, tiles)
+                nc.vector.tensor_tensor(pages[4 * b + t][:].indirect(idx3[:]), amp[:], cosine[:], ALU.mult)
 
         def examine(b, lo, hi):
             n = hi - lo
@@ -198,10 +205,10 @@ def tile_list_prior_art_scores_kernel(tc, tab_words, tab_scales, tab2_words, tab
             nc.vector.tensor_copy(words[:], tab2_sb[a][:].bitcast(U32).indirect(idx2[:]))
             return words
 
-        w1q0 = [quantise_w1(a, 0, 64) for a in range(KP)]
-        content()
-        for bt in range(4 * HP):
-            weigh(bt)
+        w1q0 = [quantise_w1(a, 0, nc.vector.tensor_copy) for a in range(KP)]
+        tanh_t = [content(b) for b in range(HP)]
+        for b in range(HP):
+            weigh(tanh_t[b])
         v2s = keep.tile([P, S2], U8, name="v2s", align_bytes=64)
         nc.vector.tensor_copy(v2s[:], tab2s_sb[:].indirect(idx2[:]))
         v2w = [gather_tab2(a) for a in range(HP)]
@@ -218,18 +225,18 @@ def tile_list_prior_art_scores_kernel(tc, tab_words, tab_scales, tab2_words, tab
         xw = [keep.tile([P, PX], U32, name="xw%d" % b, align_bytes=64) for b in range(HP)]
         xs = [keep.tile([P, PX], U8, name="xs%d" % b, align_bytes=64) for b in range(HP)]
 
-        phase_and_scatter(0, w1q0)
-        w1q1 = [quantise_w1(a, 1, P) for a in range(KP)]
+        phase_and_scatter(0, w1q0, tanh_t[0])
+        w1q1 = [quantise_w1(a, 1, nc.scalar.copy) for a in range(KP)]
         larger0 = examine(0, 0, PX)
-        phase_and_scatter(1, w1q1)
+        phase_and_scatter(1, w1q1, tanh_t[1])
         quantise_x(0, 0, PX, larger0, nc.scalar.copy)
         out_rows = out.rearrange("(m p) j -> p m j", p=P)
         for lo, hi in CHUNKS:
             quantise_x(1, lo, hi, examine(1, lo, hi), nc.scalar.copy if lo == 0 else nc.vector.tensor_copy)
             for m0 in range(0, S2 // P, 2):
-                score = keep.tile([P, 2, hi - lo], F32, name="amp", bufs=4 * HP)
+                score = keep.tile([P, 2, hi - lo], F32, name="tanh_t", bufs=4 * HP)
                 for m in range(m0, m0 + 2):
-                    acc = psum.tile([P, hi - lo], F32, name="acc")
+                    acc = psum.tile([P, hi - lo], F32, name=("wide", "turn")[m % 2])
                     for b in range(HP):
                         nc.tensor.matmul_mx(out=acc[:], lhsT=v2w[b][:, P * m : P * (m + 1)].bitcast(FP8X4),
                                             lhsT_scale=v2s[4 * b :, P * m : P * (m + 1)], rhs=xw[b][:, lo:hi].bitcast(FP8X4),

@@ -114,14 +114,8 @@ def tile_list_prior_art_scores_kernel(tc, tab_words, tab_scales, tab2_words, tab
             nc.vector.tensor_copy(plane[:], tabs_sb[:, a, :].indirect(idx[:]))
             vs.append(plane)
 
-        turned = psum.tile([P, 4, P], F32, name="turn")
-        for c in range(4):
-            nc.tensor.transpose(turned[:, c, :], wgs_sb[:, P * c : P * (c + 1)], ident[:])
-        wgs_t = keep.tile([P, 4, 4, 32], F32, name="wgs_t")
-        nc.scalar.copy(out=wgs_t[:], in_=turned[:].rearrange("p c (m t) -> p c t m", t=4))
-
         def content(b):
-            accs = [psum.tile([P, 512], F32, name=("wide", "turn")[b]) for c in range(4)]
+            accs = [psum.tile([P, 512], F32, name="turn") for c in range(4)]
             for a in range(KP):
                 for c in range(4):
                     nc.tensor.matmul_mx(out=accs[c][:], lhsT=vw[a][:, P * c : P * (c + 1)].bitcast(FP8X4),
@@ -135,10 +129,10 @@ def tile_list_prior_art_scores_kernel(tc, tab_words, tab_scales, tab2_words, tab
                 tiles.append(tile)
             return tiles
 
-        def weigh(tiles):
+        def weigh(engine, tiles):
             for c in range(4):
                 view = tiles[c][:].rearrange("p t (q m) -> p t q m", q=4)
-                nc.vector.tensor_tensor(view, view, wgs_t[:, c, :, :].unsqueeze(2).to_broadcast([P, 4, 4, 32]), ALU.mult)
+                engine.tensor_tensor(view, view, wgs_t[:, c, :, :].unsqueeze(2).to_broadcast([P, 4, 4, 32]), ALU.mult)
 
         def amplitude(b, t, tiles):
             bank = psum.tile([P, S], F32, name="turn")
@@ -206,9 +200,16 @@ def tile_list_prior_art_scores_kernel(tc, tab_words, tab_scales, tab2_words, tab
             return words
 
         w1q0 = [quantise_w1(a, 0, nc.vector.tensor_copy) for a in range(KP)]
-        tanh_t = [content(b) for b in range(HP)]
-        for b in range(HP):
-            weigh(tanh_t[b])
+        tanh_t = [content(0)]
+        turned = psum.tile([P, 4, P], F32, name="turn")
+        for c in range(4):
+            nc.tensor.transpose(turned[:, c, :], wgs_sb[:, P * c : P * (c + 1)], ident[:])
+        wgs_t = keep.tile([P, 4, 4, 32], F32, name="wgs_t")
+        nc.scalar.copy(out=wgs_t[:], in_=turned[:].rearrange("p c (m t) -> p c t m", t=4))
+
+        tanh_t.append(content(1))
+        weigh(nc.vector, tanh_t[0])
+        weigh(nc.gpsimd, tanh_t[1])
         v2s = keep.tile([P, S2], U8, name="v2s", align_bytes=64)
         nc.vector.tensor_copy(v2s[:], tab2s_sb[:].indirect(idx2[:]))
         v2w = [gather_tab2(a) for a in range(HP)]
@@ -231,15 +232,24 @@ def tile_list_prior_art_scores_kernel(tc, tab_words, tab_scales, tab2_words, tab
         phase_and_scatter(1, w1q1, tanh_t[1])
         quantise_x(0, 0, PX, larger0, nc.scalar.copy)
         out_rows = out.rearrange("(m p) j -> p m j", p=P)
+        banks = {}
+
+        def score_pass(b, lo, hi):
+            for m in range(S2 // P):
+                if (lo, m // 2) not in banks:
+                    banks[lo, m // 2] = psum.tile([P, 2, hi - lo], F32, name="turn" if lo else "wide")
+                nc.tensor.matmul_mx(out=banks[lo, m // 2][:, m % 2, :], lhsT=v2w[b][:, P * m : P * (m + 1)].bitcast(FP8X4),
+                                    lhsT_scale=v2s[4 * b :, P * m : P * (m + 1)], rhs=xw[b][:, lo:hi].bitcast(FP8X4),
+                                    rhs_scale=xs[b][:, lo:hi], start=(b == 0 and m % 2 == 0), stop=(b == HP - 1 and m % 2 == 1))
+
+        for lo, hi in CHUNKS:
+            score_pass(0, lo, hi)
         for lo, hi in CHUNKS:
             quantise_x(1, lo, hi, examine(1, lo, hi), nc.scalar.copy if lo == 0 else nc.vector.tensor_copy)
+            score_pass(1, lo, hi)
             for m0 in range(0, S2 // P, 2):
                 score = keep.tile([P, 2, hi - lo], F32, name="tanh_t", bufs=4 * HP)
                 for m in range(m0, m0 + 2):
-                    acc = psum.tile([P, hi - lo], F32, name=("wide", "turn")[m % 2])
-                    for b in range(HP):
-                        nc.tensor.matmul_mx(out=acc[:], lhsT=v2w[b][:, P * m : P * (m + 1)].bitcast(FP8X4),
-                                            lhsT_scale=v2s[4 * b :, P * m : P * (m + 1)], rhs=xw[b][:, lo:hi].bitcast(FP8X4),
-                                            rhs_scale=xs[b][:, lo:hi], start=(b == 0), stop=(b == HP - 1))
-                    nc.scalar.activation(out=score[:, m - m0, :], in_=acc[:], func=ACT.Sigmoid, scale=cand_sb[:, m : m + 1])
+                    nc.scalar.activation(out=score[:, m - m0, :], in_=banks[lo, m0 // 2][:, m - m0, :], func=ACT.Sigmoid,
+                                         scale=cand_sb[:, m : m + 1])
                 nc.sync.dma_start(out=out_rows[:, m0 : m0 + 2, lo:hi], in_=score[:])

@@ -41,6 +41,8 @@ def tile_list_prior_art_scores_kernel(tc, tab_words, tab_scales, tab2_words, tab
 
         ident = keep.tile([P, P], F32, name="ident")
         make_identity(nc, ident[:])
+        warm = keep.tile([P, 1], F32, name="warm")
+        nc.scalar.activation(out=warm[:], in_=ident[:, 0:1], func=ACT.Silu)
 
         def packed_scales(name, scales, passes, width):
             plane = keep.tile([P, width], U8, name=name, align_bytes=64)

import math
from contextlib import ExitStack

import concourse.mybir as mybir
from concourse.masks import make_identity

K, H, T, S, T2, PX, T3, S2 = 1536, 1024, 2048, 512, 1024, 512, 2048, 1024
FLOPS = 2 * (2 * K * H * S + H * S2 * PX)

F32 = mybir.dt.float32
BF16 = mybir.dt.bfloat16
I32 = mybir.dt.int32
U32 = mybir.dt.uint32
U16 = mybir.dt.uint16
U8 = mybir.dt.uint8
FP8X4 = mybir.dt.float8_e4m3fn_x4
FP4X4 = mybir.dt.float4_e2m1fn_x4
ALU = mybir.AluOpType
ACT = mybir.ActivationFunctionType

P = 128
KP = K // 512
HP = H // 512
CHUNKS = ((0, 256), (256, 512))


def tile_list_prior_art_scores_kernel(tc, tab_words, tab_scales, tab2_words, tab2_scales, w4_words, w4_scales,
                                                w1, gain, wgs, page0, cls, cand, offs, offs2, offs3, offs4, out):
    nc = tc.nc
    with ExitStack() as ctx:
        lists = ctx.enter_context(tc.tile_pool(name="lists", bufs=1))
        keep = ctx.enter_context(tc.tile_pool(name="keep", bufs=1))
        ring = ctx.enter_context(tc.tile_pool(name="ring", bufs=2))
        stage = ctx.enter_context(tc.tile_pool(name="stage", bufs=1))
        psum = ctx.enter_context(tc.psum_pool(name="psum", bufs=4))

        idx = lists.tile([P, S // 16], U16, name="idx")
        idx2 = lists.tile([P, S2 // 16], U16, name="idx2")
        idx3 = lists.tile([P, S // 16], U16, name="idx3")
        idx4 = lists.tile([P, PX // 16], U16, name="idx4")

        ident = keep.tile([P, P], F32, name="ident")
        make_identity(nc, ident[:])
        warm = keep.tile([P, 1], F32, name="warm")
        nc.scalar.activation(out=warm[:], in_=ident[:, 0:1], func=ACT.Silu)

        def packed_scales(name, scales, passes, width):
            plane = keep.tile([P, width], U8, name=name, align_bytes=64)
            nc.vector.memset(plane[:].bitcast(I32), 0)
            for q in range(4):
                nc.sync.dma_start(out=plane[32 * q : 32 * q + 4 * passes, :].bitcast(I32),
                                  in_=scales[:, 4 * q : 4 * q + 4, :].bitcast(I32))
            return plane

        def spread_scales(name, scales, width, engine):
            planes = keep.tile([P, KP, width], U8, name=name, align_bytes=64)
            engine.memset(planes[:].bitcast(I32), 0)
            for q in range(4):
                nc.sync.dma_start(out=planes[32 * q : 32 * q + 4, :, :].bitcast(I32),
                                  in_=scales[:, 4 * q : 4 * q + 4, :].rearrange("a r n -> r a n").bitcast(I32))
            return planes

        def load_words(name, words, a):
            tile = keep.tile([P, words.shape[2]], I32, name="%s%d" % (name, a), align_bytes=64)
            nc.sync.dma_start(out=tile[:], in_=words[a].rearrange("p n i -> p (n i)").bitcast(I32))
            return tile

        def load_w4(a):
            tile = keep.tile([P, 2 * H], U8, name="w4_%d" % a, align_bytes=64)
            nc.sync.dma_start(out=tile[:].bitcast(I32), in_=w4_words[a].bitcast(I32))
            return tile

        def load_w1(a, b):
            raw = ring.tile([P, 4, 512], F32, name="w1_raw", bufs=3)
            nc.sync.dma_start(out=raw[:], in_=w1[512 * a : 512 * (a + 1), 512 * b : 512 * (b + 1)].rearrange("(p j) c -> p j c", j=4))
            return raw

        def load_page(b, t):
            tile = keep.tile([P, T2], F32, name="page%d" % (4 * b + t))
            nc.sync.dma_start(out=tile[:], in_=page0[512 * b : 512 * (b + 1), :].rearrange("(p t) c -> p t c", t=4)[:, t, :])
            return tile

        def load_cls(b):
            tile = keep.tile([P, 4, PX], F32, name="cls%d" % b)
            nc.sync.dma_start(out=tile[:], in_=cls[512 * b : 512 * (b + 1), :].rearrange("(p t) j -> p t j", t=4))
            return tile

        for tile, src in ((idx, offs), (idx2, offs2), (idx3, offs3), (idx4, offs4)):
            nc.sync.dma_start(tile[:], src)
        gain_sb = keep.tile([P, HP, 4], F32, name="gain_sb")
        nc.sync.dma_start(out=gain_sb[:], in_=gain.rearrange("(b p t) -> p b t", b=HP, t=4))
        tab_sb = [load_words("tab", tab_words, 0)]
        w4_sb = [load_w4(a) for a in range(KP - 1)]
        tabs_sb = spread_scales("tabs", tab_scales, T, nc.vector)
        tab_sb.append(load_words("tab", tab_words, 1))
        w4s = spread_scales("w4s", w4_scales, H, nc.vector)
        w4_sb.append(load_w4(KP - 1))
        tab_sb.append(load_words("tab", tab_words, 2))
        w1_raw = {}
        for a in range(KP):
            w1_raw[a, 0] = load_w1(a, 0)
        wgs_sb = keep.tile([P, S], F32, name="wgs_sb")
        nc.sync.dma_start(out=wgs_sb[:], in_=wgs)
        tab2_sb = [load_words("tabb", tab2_words, 0)]
        tab2s_sb = packed_scales("tabbs", tab2_scales, HP, T3)
        pages = [load_page(0, 0)]
        tab2_sb.append(load_words("tabb", tab2_words, 1))
        pages.extend(load_page(0, t) for t in range(1, 4))

        vw, vs = [], []
        for a in range(KP):
            words = keep.tile([P, S], U32, name="vw%d" % a, align_bytes=64)
            nc.vector.tensor_copy(words[:], tab_sb[a][:].bitcast(U32).indirect(idx[:]))
            vw.append(words)
            plane = keep.tile([P, S], U8, name="vs%d" % a, align_bytes=64)
            nc.vector.tensor_copy(plane[:], tabs_sb[:, a, :].indirect(idx[:]))
            vs.append(plane)

        def content(b):
            accs = [psum.tile([P, 512], F32, name="turn") for c in range(4)]
            for a in range(KP):
                for c in range(4):
                    nc.tensor.matmul_mx(out=accs[c][:], lhsT=vw[a][:, P * c : P * (c + 1)].bitcast(FP8X4),
                                        lhsT_scale=vs[a][:, P * c : P * (c + 1)],
                                        rhs=w4_sb[a][:, 1024 * b : 1024 * (b + 1)].bitcast(FP4X4),
                                        rhs_scale=w4s[:, a, 512 * b : 512 * (b + 1)], start=(a == 0), stop=(a == KP - 1))
            tiles = []
            for c in range(4):
                tile = keep.tile([P, 4, P], F32, name="tanh_t", bufs=4 * HP)
                nc.scalar.activation(out=tile[:], in_=accs[c][:].rearrange("p (m t) -> p t m", t=4), func=ACT.Tanh)
                tiles.append(tile)
            return tiles

        def weigh(engine, tiles):
            for c in range(4):
                view = tiles[c][:].rearrange("p t (q m) -> p t q m", q=4)
                engine.tensor_tensor(view, view, wgs_t[:, c, :, :].unsqueeze(2).to_broadcast([P, 4, 4, 32]), ALU.mult)

        def amplitude(b, t, tiles):
            bank = psum.tile([P, S], F32, name="turn")
            for c in range(4):
                nc.tensor.transpose(bank[:, P * c : P * (c + 1)], tiles[c][:, t, :], ident[:])
            tile = ring.tile([P, S], F32, name="amp", bufs=4)
            nc.scalar.activation(out=tile[:], in_=bank[:], func=ACT.Copy, scale=gain_sb[:, b, t : t + 1])
            return tile

        def quantise_w1(a, b, weave):
            grouped = stage.tile([P, 2048], BF16, name="grouped%d%d" % (a, b), align_bytes=64, offset=4096 * ((a + b) % 2))
            dst = grouped[:].rearrange("p (m i j) -> p m j i", i=4, j=4)
            raw = w1_raw[a, b][:].rearrange("p j (m i) -> p m j i", i=4)
            weave(out=dst, in_=raw)
            codes = keep.tile([P, 512], U32, name="w1c%d%d" % (a, b), align_bytes=64)
            scales = keep.tile([P, 512], U8, name="w1s%d%d" % (a, b), align_bytes=64)
            nc.vector.quantize_mx(out=codes[:].bitcast(FP8X4), scales=scales[:], in_=grouped[:])
            return codes, scales

        def phase_and_scatter(b, w1q, tiles):
            accs = [psum.tile([P, 512], F32, name="wide") for c in range(4)]
            for a in range(KP):
                codes, scales = w1q[a]
                for c in range(4):
                    nc.tensor.matmul_mx(out=accs[c][:], lhsT=vw[a][:, P * c : P * (c + 1)].bitcast(FP8X4),
                                        lhsT_scale=vs[a][:, P * c : P * (c + 1)], rhs=codes[:].bitcast(FP8X4),
                                        rhs_scale=scales[:], start=(a == 0), stop=(a == KP - 1))
            for t in range(4):
                turns = ring.tile([P, S], F32, name="turns")
                for c in range(4):
                    nc.scalar.activation(out=turns[:, P * c : P * (c + 1)], in_=accs[c][:, t::4], func=ACT.Abs,
                                         scale=1.0 / (2.0 * math.pi))
                whole = stage.tile([P, S], U32, name="whole%d%d" % (b, t), align_bytes=64, offset=12288 + 2048 * (t % 2))
                nc.scalar.activation(out=whole[:], in_=turns[:], func=ACT.Copy, bias=0.25)
                shift = ring.tile([P, S], F32, name="shift")
                nc.scalar.activation(out=shift[:], in_=whole[:], func=ACT.Copy, scale=-1.0, bias=0.25)
                reduced = psum.tile([P, S], F32, name="turn")
                for c in range(4):
                    cols = slice(P * c, P * (c + 1))
                    nc.tensor.matmul(reduced[:, cols], lhsT=turns[:, cols], rhs=ident[:], start=True, stop=False, is_transpose=True)
                    nc.tensor.matmul(reduced[:, cols], lhsT=shift[:, cols], rhs=ident[:], start=False, stop=True, is_transpose=True)
                cosine = ring.tile([P, S], F32, name="cosine", bufs=4)
                nc.scalar.activation(out=cosine[:], in_=reduced[:], func=ACT.Sin, scale=2.0 * math.pi)
                amp = amplitude(b, t, tiles)
                nc.vector.tensor_tensor(pages[4 * b + t][:].indirect(idx3[:]), amp[:], cosine[:], ALU.mult)

        def examine(b, lo, hi):
            n = hi - lo
            picked = stage.tile([P, 4, n], F32, name="picked%d%d" % (b, lo), align_bytes=64, offset=0)
            larger = stage.tile([P, 4, n], BF16, name="larger%d%d" % (b, lo), align_bytes=64, offset=(4096 if b else 8192) + 8 * lo)
            for t in range(4):
                nc.vector.tensor_copy(picked[:, t, :], pages[4 * b + t][:].indirect(idx4[:, lo // 16 : hi // 16]))
            for t0, t1 in ((0, 3), (3, 4)):
                nc.vector.tensor_tensor(larger[:, t0:t1, :], picked[:, t0:t1, :], cls_sb[b][:, t0:t1, lo:hi], ALU.max)
            return larger

        def quantise_x(b, lo, hi, larger, weave):
            x = stage.tile([P, 4 * (hi - lo)], BF16, name="x%d%d" % (b, lo), align_bytes=64, offset=12288 + 8 * lo)
            weave(out=x[:].rearrange("p (c i t) -> p c t i", t=4, i=4), in_=larger[:].rearrange("p t (c i) -> p c t i", i=4))
            nc.vector.quantize_mx(out=xw[b][:, lo:hi].bitcast(FP8X4), scales=xs[b][:, lo:hi], in_=x[:])

        def gather_tab2(a):
            words = keep.tile([P, S2], U32, name="v2w%d" % a, align_bytes=64)
            nc.vector.tensor_copy(words[:], tab2_sb[a][:].bitcast(U32).indirect(idx2[:]))
            return words

        w1q0 = [quantise_w1(a, 0, nc.vector.tensor_copy) for a in range(KP)]
        tanh_t = [content(0)]
        turned = psum.tile([P, 4, P], F32, name="turn")
        for c in range(4):
            nc.tensor.transpose(turned[:, c, :], wgs_sb[:, P * c : P * (c + 1)], ident[:])
        wgs_t = keep.tile([P, 4, 4, 32], F32, name="wgs_t")
        nc.scalar.copy(out=wgs_t[:], in_=turned[:].rearrange("p c (m t) -> p c t m", t=4))

        tanh_t.append(content(1))
        weigh(nc.vector, tanh_t[0])
        weigh(nc.gpsimd, tanh_t[1])
        v2s = keep.tile([P, S2], U8, name="v2s", align_bytes=64)
        nc.vector.tensor_copy(v2s[:], tab2s_sb[:].indirect(idx2[:]))
        v2w = [gather_tab2(a) for a in range(HP)]

        for a in range(KP):
            w1_raw[a, 1] = load_w1(a, 1)
        cls_sb = [load_cls(0)]
        pages.extend(load_page(1, t) for t in range(4))
        cls_sb.append(load_cls(1))
        cand_sb = keep.tile([P, S2 // P], F32, name="cand_sb")
        with nc.allow_non_contiguous_dma(reason="one factor to a partition"):
            nc.sync.dma_start(out=cand_sb[:], in_=cand.rearrange("(m p) -> p m", p=P))

        xw = [keep.tile([P, PX], U32, name="xw%d" % b, align_bytes=64) for b in range(HP)]
        xs = [keep.tile([P, PX], U8, name="xs%d" % b, align_bytes=64) for b in range(HP)]

        phase_and_scatter(0, w1q0, tanh_t[0])
        w1q1 = [quantise_w1(a, 1, nc.scalar.copy) for a in range(KP)]
        larger0 = examine(0, 0, PX)
        phase_and_scatter(1, w1q1, tanh_t[1])
        quantise_x(0, 0, PX, larger0, nc.scalar.copy)
        out_rows = out.rearrange("(m p) j -> p m j", p=P)
        banks = {}

        def score_pass(b, lo, hi):
            for m in range(S2 // P):
                if (lo, m // 2) not in banks:
                    banks[lo, m // 2] = psum.tile([P, 2, hi - lo], F32, name="turn" if lo else "wide")
                nc.tensor.matmul_mx(out=banks[lo, m // 2][:, m % 2, :], lhsT=v2w[b][:, P * m : P * (m + 1)].bitcast(FP8X4),
                                    lhsT_scale=v2s[4 * b :, P * m : P * (m + 1)], rhs=xw[b][:, lo:hi].bitcast(FP8X4),
                                    rhs_scale=xs[b][:, lo:hi], start=(b == 0 and m % 2 == 0), stop=(b == HP - 1 and m % 2 == 1))

        for lo, hi in CHUNKS:
            score_pass(0, lo, hi)
        for lo, hi in CHUNKS:
            quantise_x(1, lo, hi, examine(1, lo, hi), nc.scalar.copy if lo == 0 else nc.vector.tensor_copy)
            score_pass(1, lo, hi)
            for m0 in range(0, S2 // P, 2):
                score = keep.tile([P, 2, hi - lo], F32, name="tanh_t", bufs=4 * HP)
                for m in range(m0, m0 + 2):
                    nc.scalar.activation(out=score[:, m - m0, :], in_=banks[lo, m0 // 2][:, m - m0, :], func=ACT.Sigmoid,
                                         scale=cand_sb[:, m : m + 1])
                nc.sync.dma_start(out=out_rows[:, m0 : m0 + 2, lo:hi], in_=score[:])
